import numpy as np
import ml_dtypes


def mxq(x, axis, fmt="e4m3"):
    dtype, down = {"e4m3": (ml_dtypes.float8_e4m3fn, 7), "e5m2": (ml_dtypes.float8_e5m2, 14)}[fmt]
    v = np.moveaxis(np.asarray(x, np.float32).astype(ml_dtypes.bfloat16).astype(np.float64), axis, -1)
    blocks = v.reshape(v.shape[:-1] + (-1, 32))
    amax = np.abs(blocks).max(-1, keepdims=True)
    byte = np.maximum(np.where(amax > 0, np.frexp(amax)[1] - 1 + 127, 0) - down, 1)
    scale = np.exp2(byte - 127.0)
    codes = (blocks / scale).astype(np.float32).astype(dtype).astype(np.float64)
    return np.moveaxis((codes * scale).reshape(v.shape), -1, axis)


WIDE = False


def mx_kscale(k):
    if not WIDE:
        return np.ones(k)
    levels = np.array([10, -10, 5, -5, 0])
    if k % 512:
        return np.exp2(np.random.permutation(np.resize(levels, k // 32))).repeat(32)
    a = np.empty((k // 512, 16))
    for p in range(k // 512):
        a[p, :8] = np.random.permutation(np.resize(levels, 8))
        for g in range(8):
            far = levels[np.abs(levels - a[p, g]) >= 10]
            a[p, g + 8] = far[np.random.randint(len(far))]
    return np.exp2(a.ravel()).repeat(32)


def f64(x):
    return np.asarray(x).astype(np.float64)


def striped8(idx):
    return np.asarray(idx).reshape(8, -1, 16).transpose(0, 2, 1).reshape(128, -1).astype(np.uint16)


def unstriped8(offs):
    return offs.reshape(8, 16, -1).transpose(0, 2, 1).reshape(8, -1).astype(np.int64)


def pick8(x, idx, run):
    r = np.arange(len(x))
    return x[r[:, None], idx[r % (8 * run) // run]]


E2M1 = np.array([0.0, 0.5, 1.0, 1.5, 2.0, 3.0, 4.0, 6.0, -0.0, -0.5, -1.0, -1.5, -2.0, -3.0, -4.0, -6.0])


def pack_weight(w, fmt):
    k, n = w.shape
    w = f64(np.asarray(w, np.float32).astype(ml_dtypes.bfloat16)).reshape(k // 32, 32, n)
    amax = np.abs(w).max(1)
    if fmt == "e4m3":
        byte = np.frexp(amax)[1] - 1 + 127 - 7
    else:
        mant, ex = np.frexp(amax / 6.0)
        byte = np.where(mant > 0.5, ex, ex - 1) + 127
    byte = np.clip(np.where(amax > 0, byte, 1), 1, 254)
    scaled = (w * np.exp2(127.0 - byte)[:, None, :]).reshape(k, n).astype(np.float32)
    by_word = np.ascontiguousarray(scaled.reshape(k // 512, 128, 4, n).transpose(0, 1, 3, 2))
    if fmt == "e4m3":
        words = by_word.astype(ml_dtypes.float8_e4m3fn).view(np.uint8)
    else:
        c = by_word.astype(ml_dtypes.float4_e2m1fn).view(np.uint8) & 0xF
        words = (c[..., 0::2] | (c[..., 1::2] << 4)).reshape(k // 512, 128, 2 * n)
    return np.ascontiguousarray(words), np.ascontiguousarray(byte.astype(np.uint8).reshape(k // 512, 16, n))


def unpack_weight(words, scales, fmt):
    g, _, n = scales.shape
    words = np.ascontiguousarray(words).reshape(g, 128, n, -1)
    if fmt == "e4m3":
        vals = words.view(ml_dtypes.float8_e4m3fn).astype(np.float64)
    else:
        nib = np.empty((g, 128, n, 4), np.uint8)
        nib[..., 0::2] = words & 0xF
        nib[..., 1::2] = words >> 4
        vals = E2M1[nib]
    vals = vals * np.repeat(np.exp2(scales.astype(np.float64) - 127.0), 8, axis=1)[..., None]
    return vals.transpose(0, 1, 3, 2).reshape(g * 512, n)


D, T, I, Q = 512, 1024, 512, 128


def setup_inputs():
    n = np.random.standard_normal
    idx = np.stack([np.random.permutation(T)[:I] for _ in range(8)])
    idx2 = np.stack([np.random.permutation(T)[:I] for _ in range(8)])
    idx3 = np.stack([np.random.permutation(T)[:I] for _ in range(8)])
    idx4 = np.stack([np.random.permutation(T)[:I] for _ in range(8)])
    fd = mx_kscale(D)
    keysp = pack_weight(n((D, T)) / fd[:, None], "e2m1")
    return {
        "query": (n((D, Q)) * 1.2 / np.sqrt(D) * fd[:, None]).astype(np.float32),
        "keys_words": keysp[0],
        "keys_scales": keysp[1],
        "lam": (np.random.uniform(0.8, 1.8, (Q, 1))).astype(np.float32),
        "averse": (np.random.uniform(0.4, 1.0, (Q, 1))).astype(np.float32),
        "old": (np.random.uniform(0.0, 2.0, (Q, T))).astype(np.float32),
        "gainm": (np.random.uniform(0.5, 1.5, (Q, I))).astype(np.float32),
        "offs": striped8(idx),
        "offs2": striped8(idx2),
        "offs3": striped8(idx3),
        "offs4": striped8(idx4),
    }


def reference(query, keys_words, keys_scales, lam, averse, old, gainm, offs, offs2, offs3, offs4):
    idx = unstriped8(offs)
    idx2 = unstriped8(offs2)
    idx3 = unstriped8(offs3)
    idx4 = unstriped8(offs4)
    keysu = unpack_weight(keys_words, keys_scales, "e2m1")
    queryq = mxq(f64(query), 0, "e4m3")
    a = queryq.T @ keysu
    lo2 = np.minimum(pick8(a, idx, 16), pick8(a, idx2, 16))
    hi2 = np.maximum(pick8(a, idx, 16), pick8(a, idx2, 16))
    s = np.maximum(lo2, np.minimum(hi2, pick8(a, idx3, 16))) * f64(lam)
    p = np.exp(s - np.max(s, axis=1, keepdims=True))
    r = p / np.sum(p, axis=1, keepdims=True)
    p2 = np.exp(s * (-1.0) - np.max(s * (-1.0), axis=1, keepdims=True))
    r2 = p2 / np.sum(p2, axis=1, keepdims=True)
    w = r - r2 * f64(averse)
    ws = w * f64(gainm) * 256.0
    wf = np.zeros((Q, T))
    wf[np.arange(Q)[:, None], idx4[np.arange(Q) % 128 // 16]] = ws
    y = f64(old) + wf
    return y

@@ -1,0 +1,157 @@
+from contextlib import ExitStack
+
+import concourse.mybir as mybir
+
+D, T, I, Q = 512, 1024, 512, 128
+FLOPS = 2 * D * Q * T
+
+F32 = mybir.dt.float32
+BF16 = mybir.dt.bfloat16
+I32 = mybir.dt.int32
+U32 = mybir.dt.uint32
+U16 = mybir.dt.uint16
+U8 = mybir.dt.uint8
+FP8X4 = mybir.dt.float8_e4m3fn_x4
+FP4X4 = mybir.dt.float4_e2m1fn_x4
+ALU = mybir.AluOpType
+ACT = mybir.ActivationFunctionType
+AX = mybir.AxisListType
+
+P = 128
+PACK = 4
+N_TILE = 256
+HALF = I // 2
+OUT_TILE = 256
+
+
+def tile_attend_middle_twoside_moved_heads_kernel(
+    tc, query, keys_words, keys_scales, lam, averse, old, gainm, offs, offs2, offs3, offs4, out
+):
+    nc = tc.nc
+    with ExitStack() as ctx:
+        sb = ctx.enter_context(tc.tile_pool(name="sb", bufs=1))
+        ps = ctx.enter_context(tc.psum_pool(name="ps", bufs=1))
+
+        k_scales = sb.tile([P, T], U8, name="k_scales", align_bytes=64)
+        nc.vector.memset(k_scales[:].bitcast(I32), 0)
+
+        q_raw = sb.tile([P, PACK, Q], F32, name="q_raw", tag="raw_then_old")
+        nc.sync.dma_start(out=q_raw[:], in_=query.rearrange("(p j) q -> p j q", j=PACK))
+        k_words = sb.tile([P, 2 * T], U8, name="k_words", align_bytes=64)
+        nc.sync.dma_start(out=k_words[:].bitcast(I32), in_=keys_words[0].bitcast(I32))
+        for quad in range(4):
+            nc.sync.dma_start(
+                out=k_scales[32 * quad : 32 * quad + 4, :].bitcast(I32),
+                in_=keys_scales[0, 4 * quad : 4 * quad + 4, :].bitcast(I32),
+            )
+        lists = []
+        for n, src in enumerate((offs, offs2, offs3, offs4)):
+            lst = sb.tile([P, I // 16], U16, name="list%d" % n)
+            nc.sync.dma_start(lst[:], src)
+            lists.append(lst)
+
+        wf = sb.tile([P, T], F32, name="wf")
+        nc.vector.memset(wf[:], 0.0)
+
+        q_bf = sb.tile([P, Q, PACK], BF16, name="q_bf", tag="bf_then_gain", align_bytes=64)
+        nc.vector.tensor_copy(
+            out=q_bf[:].rearrange("p (c i) j -> p c j i", i=4),
+            in_=q_raw[:].rearrange("p j (c i) -> p c j i", i=4),
+        )
+        q_codes = sb.tile([P, Q], U32, name="q_codes", tag="codes_then_lam", align_bytes=64)
+        q_scales = sb.tile([P, Q], U8, name="q_scales", tag="scales_then_averse", align_bytes=64)
+        nc.vector.quantize_mx(
+            out=q_codes[:].bitcast(FP8X4),
+            scales=q_scales[:],
+            in_=q_bf[:].rearrange("p q j -> p (q j)"),
+        )
+
+        old_t = sb.tile([P, T], F32, name="old_t", tag="raw_then_old")
+        nc.sync.dma_start(out=old_t[:], in_=old)
+        gain_t = sb.tile([P, I], F32, name="gain_t", tag="bf_then_gain", align_bytes=64)
+        nc.sync.dma_start(out=gain_t[:], in_=gainm)
+
+        a = sb.tile([P, T], F32, name="a", tag="a_then_gain")
+        for b in range(T // N_TILE):
+            cols = slice(b * N_TILE, (b + 1) * N_TILE)
+            bank = ps.tile([P, N_TILE], F32, name="bank%d" % b)
+            nc.tensor.matmul_mx(
+                out=bank[:],
+                lhsT=q_codes[:].bitcast(FP8X4),
+                lhsT_scale=q_scales[:],
+                rhs=k_words[:, 2 * b * N_TILE : 2 * (b + 1) * N_TILE].bitcast(FP4X4),
+                rhs_scale=k_scales[:, cols],
+                start=True,
+                stop=True,
+            )
+            if b % 2 == 0:
+                nc.scalar.activation(out=a[:, cols], in_=bank[:], func=ACT.Copy)
+            else:
+                nc.vector.tensor_copy(out=a[:, cols], in_=bank[:])
+
+        lam_t = sb.tile([P, 1], F32, name="lam_t", tag="codes_then_lam", align_bytes=64)
+        nc.sync.dma_start(out=lam_t[:], in_=lam)
+        averse_t = sb.tile([P, 1], F32, name="averse_t", tag="scales_then_averse", align_bytes=64)
+        nc.sync.dma_start(out=averse_t[:], in_=averse)
+
+        halves = [slice(0, HALF), slice(HALF, I)]
+        list_halves = [slice(0, HALF // 16), slice(HALF // 16, I // 16)]
+
+        x = sb.tile([P, I], F32, name="x")
+        y = sb.tile([P, I], F32, name="y")
+        z = sb.tile([P, I], F32, name="z")
+        nc.scalar.activation(out=x[:], in_=a[:].indirect(lists[0][:]), func=ACT.Copy)
+        nc.vector.tensor_copy(out=y[:], in_=a[:].indirect(lists[1][:]))
+        for h in range(2):
+            nc.scalar.activation(
+                out=z[:, halves[h]], in_=a[:].indirect(lists[2][:, list_halves[h]]), func=ACT.Copy
+            )
+
+        gain256 = sb.tile([P, I], F32, name="gain256", tag="a_then_gain")
+        nc.scalar.activation(out=gain256[:], in_=gain_t[:], func=ACT.Copy, scale=256.0)
+
+        hi = sb.tile([P, I], F32, name="hi")
+        lo = sb.tile([P, I], F32, name="lo")
+        cap = sb.tile([P, I], F32, name="cap")
+        mid = sb.tile([P, I], F32, name="mid")
+        nc.vector.tensor_tensor(out=hi[:], in0=x[:], in1=y[:], op=ALU.max)
+        nc.vector.tensor_tensor(out=lo[:], in0=x[:], in1=y[:], op=ALU.min)
+        for h in halves:
+            nc.vector.tensor_tensor(out=cap[:, h], in0=hi[:, h], in1=z[:, h], op=ALU.min)
+        for h in halves:
+            nc.vector.tensor_tensor(out=mid[:, h], in0=lo[:, h], in1=cap[:, h], op=ALU.max)
+
+        s = sb.tile([P, I], F32, name="s")
+        s_min = sb.tile([P, 1], F32, name="s_min")
+        nc.vector.tensor_scalar(
+            out=s[:], in0=mid[:], scalar1=lam_t[:], scalar2=None, op0=ALU.mult, op1=ALU.min, accum_out=s_min[:]
+        )
+        neg_max = sb.tile([P, 1], F32, name="neg_max")
+        nc.vector.tensor_reduce(out=neg_max[:], in_=s[:], axis=AX.X, op=ALU.max, negate=True)
+
+        p2 = sb.tile([P, I], F32, name="p2")
+        sum2 = sb.tile([P, 1], F32, name="sum2")
+        nc.scalar.activation(out=p2[:], in_=s[:], func=ACT.Exp, bias=s_min[:], scale=-1.0, accum_out=sum2[:])
+        p1 = sb.tile([P, I], F32, name="p1")
+        sum1 = sb.tile([P, 1], F32, name="sum1")
+        nc.scalar.activation(out=p1[:], in_=s[:], func=ACT.Exp, bias=neg_max[:], scale=1.0, accum_out=sum1[:])
+
+        inv2 = sb.tile([P, 1], F32, name="inv2")
+        nc.vector.reciprocal(out=inv2[:], in_=sum2[:])
+        r2a = sb.tile([P, I], F32, name="r2a")
+        nc.vector.tensor_scalar(
+            out=r2a[:], in0=p2[:], scalar1=inv2[:], scalar2=averse_t[:], op0=ALU.mult, op1=ALU.mult
+        )
+        inv1 = sb.tile([P, 1], F32, name="inv1")
+        nc.vector.reciprocal(out=inv1[:], in_=sum1[:])
+        w = sb.tile([P, I], F32, name="w")
+        nc.vector.scalar_tensor_tensor(
+            out=w[:], in0=p1[:], scalar=inv1[:], in1=r2a[:], op0=ALU.mult, op1=ALU.subtract
+        )
+        nc.vector.tensor_tensor(out=wf[:].indirect(lists[3][:]), in0=w[:], in1=gain256[:], op=ALU.mult)
+
+        for c in range(T // OUT_TILE):
+            cols = slice(c * OUT_TILE, (c + 1) * OUT_TILE)
+            res = sb.tile([P, OUT_TILE], F32, name="res%d" % c)
+            nc.vector.tensor_tensor(out=res[:], in0=old_t[:, cols], in1=wf[:, cols], op=ALU.add)
+            nc.sync.dma_start(out=out[:, cols], in_=res[:])

@@ -72,19 +72,20 @@ def tile_attend_middle_twoside_moved_heads_kernel(
         nc.sync.dma_start(out=gain_t[:], in_=gainm)
 
         a = sb.tile([P, T], F32, name="a", tag="a_then_gain")
-        for b in range(T // N_TILE):
-            cols = slice(b * N_TILE, (b + 1) * N_TILE)
-            bank = ps.tile([P, N_TILE], F32, name="bank%d" % b)
+        edges = (0, 512, 768, 896, 1024)
+        for b in range(4):
+            cols = slice(edges[b], edges[b + 1])
+            bank = ps.tile([P, edges[b + 1] - edges[b]], F32, name="bank%d" % b)
             nc.tensor.matmul_mx(
                 out=bank[:],
                 lhsT=q_codes[:].bitcast(FP8X4),
                 lhsT_scale=q_scales[:],
-                rhs=k_words[:, 2 * b * N_TILE : 2 * (b + 1) * N_TILE].bitcast(FP4X4),
+                rhs=k_words[:, 2 * edges[b] : 2 * edges[b + 1]].bitcast(FP4X4),
                 rhs_scale=k_scales[:, cols],
                 start=True,
                 stop=True,
             )
-            if b % 2 == 0:
+            if b in (0, 3):
                 nc.scalar.activation(out=a[:, cols], in_=bank[:], func=ACT.Copy)
             else:
                 nc.vector.tensor_copy(out=a[:, cols], in_=bank[:])
@@ -100,22 +101,26 @@ def tile_attend_middle_twoside_moved_heads_kernel(
         x = sb.tile([P, I], F32, name="x")
         y = sb.tile([P, I], F32, name="y")
         z = sb.tile([P, I], F32, name="z")
-        nc.scalar.activation(out=x[:], in_=a[:].indirect(lists[0][:]), func=ACT.Copy)
-        nc.vector.tensor_copy(out=y[:], in_=a[:].indirect(lists[1][:]))
         for h in range(2):
-            nc.scalar.activation(
-                out=z[:, halves[h]], in_=a[:].indirect(lists[2][:, list_halves[h]]), func=ACT.Copy
-            )
+            nc.vector.tensor_copy(out=y[:, halves[h]], in_=a[:].indirect(lists[1][:, list_halves[h]]))
+        for dst, lst in ((x, lists[0]), (z, lists[2])):
+            for h in range(2):
+                nc.scalar.activation(
+                    out=dst[:, halves[h]], in_=a[:].indirect(lst[:, list_halves[h]]), func=ACT.Copy
+                )
 
         gain256 = sb.tile([P, I], F32, name="gain256", tag="a_then_gain")
         nc.scalar.activation(out=gain256[:], in_=gain_t[:], func=ACT.Copy, scale=256.0)
+        neg_lam = sb.tile([P, 1], F32, name="neg_lam")
+        nc.scalar.activation(out=neg_lam[:], in_=lam_t[:], func=ACT.Copy, scale=-1.0)
 
         hi = sb.tile([P, I], F32, name="hi")
         lo = sb.tile([P, I], F32, name="lo")
         cap = sb.tile([P, I], F32, name="cap")
         mid = sb.tile([P, I], F32, name="mid")
-        nc.vector.tensor_tensor(out=hi[:], in0=x[:], in1=y[:], op=ALU.max)
-        nc.vector.tensor_tensor(out=lo[:], in0=x[:], in1=y[:], op=ALU.min)
+        for h in halves:
+            nc.vector.tensor_tensor(out=hi[:, h], in0=x[:, h], in1=y[:, h], op=ALU.max)
+            nc.vector.tensor_tensor(out=lo[:, h], in0=x[:, h], in1=y[:, h], op=ALU.min)
         for h in halves:
             nc.vector.tensor_tensor(out=cap[:, h], in0=hi[:, h], in1=z[:, h], op=ALU.min)
         for h in halves:
@@ -127,14 +132,17 @@ def tile_attend_middle_twoside_moved_heads_kernel(
             out=s[:], in0=mid[:], scalar1=lam_t[:], scalar2=None, op0=ALU.mult, op1=ALU.min, accum_out=s_min[:]
         )
         neg_max = sb.tile([P, 1], F32, name="neg_max")
-        nc.vector.tensor_reduce(out=neg_max[:], in_=s[:], axis=AX.X, op=ALU.max, negate=True)
+        neg_s = sb.tile([P, I], F32, name="neg_s")
+        nc.vector.tensor_scalar(
+            out=neg_s[:], in0=mid[:], scalar1=neg_lam[:], scalar2=None, op0=ALU.mult, op1=ALU.min, accum_out=neg_max[:]
+        )
 
         p2 = sb.tile([P, I], F32, name="p2")
         sum2 = sb.tile([P, 1], F32, name="sum2")
         nc.scalar.activation(out=p2[:], in_=s[:], func=ACT.Exp, bias=s_min[:], scale=-1.0, accum_out=sum2[:])
         p1 = sb.tile([P, I], F32, name="p1")
         sum1 = sb.tile([P, 1], F32, name="sum1")
-        nc.scalar.activation(out=p1[:], in_=s[:], func=ACT.Exp, bias=neg_max[:], scale=1.0, accum_out=sum1[:])
+        nc.scalar.activation(out=p1[:], in_=neg_s[:], func=ACT.Exp, bias=neg_max[:], scale=-1.0, accum_out=sum1[:])
 
         inv2 = sb.tile([P, 1], F32, name="inv2")
         nc.vector.reciprocal(out=inv2[:], in_=sum2[:])
@@ -150,8 +158,9 @@ def tile_attend_middle_twoside_moved_heads_kernel(
         )
         nc.vector.tensor_tensor(out=wf[:].indirect(lists[3][:]), in0=w[:], in1=gain256[:], op=ALU.mult)
 
-        for c in range(T // OUT_TILE):
-            cols = slice(c * OUT_TILE, (c + 1) * OUT_TILE)
-            res = sb.tile([P, OUT_TILE], F32, name="res%d" % c)
+        out_edges = (0, 128, 384, 640, 896, 1024)
+        for c in range(5):
+            cols = slice(out_edges[c], out_edges[c + 1])
+            res = sb.tile([P, out_edges[c + 1] - out_edges[c]], F32, name="res%d" % c)
             nc.vector.tensor_tensor(out=res[:], in0=old_t[:, cols], in1=wf[:, cols], op=ALU.add)
             nc.sync.dma_start(out=out[:, cols], in_=res[:])

@@ -33,17 +33,17 @@ def tile_attend_middle_twoside_moved_heads_kernel(
         ps = ctx.enter_context(tc.psum_pool(name="ps", bufs=1))
 
         k_scales = sb.tile([P, T], U8, name="k_scales", align_bytes=64)
-        nc.vector.memset(k_scales[:].bitcast(I32), 0)
 
         q_raw = sb.tile([P, PACK, Q], F32, name="q_raw", tag="raw_then_old")
         nc.sync.dma_start(out=q_raw[:], in_=query.rearrange("(p j) q -> p j q", j=PACK))
-        k_words = sb.tile([P, 2 * T], U8, name="k_words", align_bytes=64)
-        nc.sync.dma_start(out=k_words[:].bitcast(I32), in_=keys_words[0].bitcast(I32))
+        k_words = [sb.tile([P, T], U8, name="k_words%d" % h, align_bytes=64) for h in range(2)]
+        nc.sync.dma_start(out=k_words[0][:].bitcast(I32), in_=keys_words[0, :, 0:T].bitcast(I32))
         for quad in range(4):
             nc.sync.dma_start(
                 out=k_scales[32 * quad : 32 * quad + 4, :].bitcast(I32),
                 in_=keys_scales[0, 4 * quad : 4 * quad + 4, :].bitcast(I32),
             )
+        nc.sync.dma_start(out=k_words[1][:].bitcast(I32), in_=keys_words[0, :, T : 2 * T].bitcast(I32))
         lists = []
         for n, src in enumerate((offs, offs2, offs3, offs4)):
             lst = sb.tile([P, I // 16], U16, name="list%d" % n)
@@ -55,8 +55,13 @@ def tile_attend_middle_twoside_moved_heads_kernel(
 
         q_bf = sb.tile([P, Q, PACK], BF16, name="q_bf", tag="bf_then_gain", align_bytes=64)
         nc.vector.tensor_copy(
-            out=q_bf[:].rearrange("p (c i) j -> p c j i", i=4),
-            in_=q_raw[:].rearrange("p j (c i) -> p c j i", i=4),
+            out=q_bf[:, 0:88, :].rearrange("p (c i) j -> p c j i", i=4),
+            in_=q_raw[:, :, 0:88].rearrange("p j (c i) -> p c j i", i=4),
+        )
+        nc.scalar.activation(
+            out=q_bf[:, 88:128, :].rearrange("p (c i) j -> p c j i", i=4),
+            in_=q_raw[:, :, 88:128].rearrange("p j (c i) -> p c j i", i=4),
+            func=ACT.Copy,
         )
         q_codes = sb.tile([P, Q], U32, name="q_codes", tag="codes_then_lam", align_bytes=64)
         q_scales = sb.tile([P, Q], U8, name="q_scales", tag="scales_then_averse", align_bytes=64)
@@ -80,7 +85,7 @@ def tile_attend_middle_twoside_moved_heads_kernel(
                 out=bank[:],
                 lhsT=q_codes[:].bitcast(FP8X4),
                 lhsT_scale=q_scales[:],
-                rhs=k_words[:, 2 * edges[b] : 2 * edges[b + 1]].bitcast(FP4X4),
+                rhs=k_words[edges[b] // 512][:, 2 * edges[b] % T : 2 * edges[b] % T + 2 * (edges[b + 1] - edges[b])].bitcast(FP4X4),
                 rhs_scale=k_scales[:, cols],
                 start=True,
                 stop=True,
@@ -163,4 +168,5 @@ def tile_attend_middle_twoside_moved_heads_kernel(
             cols = slice(out_edges[c], out_edges[c + 1])
             res = sb.tile([P, out_edges[c + 1] - out_edges[c]], F32, name="res%d" % c)
             nc.vector.tensor_tensor(out=res[:], in0=old_t[:, cols], in1=wf[:, cols], op=ALU.add)
-            nc.sync.dma_start(out=out[:, cols], in_=res[:])
+            queue = nc.sync if c % 2 == 0 else nc.scalar
+            queue.dma_start(out=out[:, cols], in_=res[:])

from contextlib import ExitStack

import concourse.mybir as mybir

D, T, I, Q = 512, 1024, 512, 128
FLOPS = 2 * D * Q * T

F32 = mybir.dt.float32
BF16 = mybir.dt.bfloat16
I32 = mybir.dt.int32
U32 = mybir.dt.uint32
U16 = mybir.dt.uint16
U8 = mybir.dt.uint8
FP8X4 = mybir.dt.float8_e4m3fn_x4
FP4X4 = mybir.dt.float4_e2m1fn_x4
ALU = mybir.AluOpType
ACT = mybir.ActivationFunctionType
AX = mybir.AxisListType

P = 128
PACK = 4
N_TILE = 256
HALF = I // 2
OUT_TILE = 256


def tile_attend_middle_twoside_moved_heads_kernel(
    tc, query, keys_words, keys_scales, lam, averse, old, gainm, offs, offs2, offs3, offs4, out
):
    nc = tc.nc
    with ExitStack() as ctx:
        sb = ctx.enter_context(tc.tile_pool(name="sb", bufs=1))
        ps = ctx.enter_context(tc.psum_pool(name="ps", bufs=1))

        k_scales = sb.tile([P, T], U8, name="k_scales", align_bytes=64)

        q_raw = sb.tile([P, PACK, Q], F32, name="q_raw", tag="raw_then_old")
        nc.sync.dma_start(out=q_raw[:], in_=query.rearrange("(p j) q -> p j q", j=PACK))
        k_words = [sb.tile([P, T], U8, name="k_words%d" % h, align_bytes=64) for h in range(2)]
        nc.sync.dma_start(out=k_words[0][:].bitcast(I32), in_=keys_words[0, :, 0:T].bitcast(I32))
        for quad in range(4):
            nc.sync.dma_start(
                out=k_scales[32 * quad : 32 * quad + 4, :].bitcast(I32),
                in_=keys_scales[0, 4 * quad : 4 * quad + 4, :].bitcast(I32),
            )
        nc.sync.dma_start(out=k_words[1][:].bitcast(I32), in_=keys_words[0, :, T : 2 * T].bitcast(I32))
        lists = []
        for n, src in enumerate((offs, offs2, offs3, offs4)):
            lst = sb.tile([P, I // 16], U16, name="list%d" % n)
            nc.sync.dma_start(lst[:], src)
            lists.append(lst)

        wf = sb.tile([P, T], F32, name="wf")
        nc.vector.memset(wf[:], 0.0)

        q_bf = sb.tile([P, Q, PACK], BF16, name="q_bf", tag="bf_then_gain", align_bytes=64)
        nc.vector.tensor_copy(
            out=q_bf[:, 0:88, :].rearrange("p (c i) j -> p c j i", i=4),
            in_=q_raw[:, :, 0:88].rearrange("p j (c i) -> p c j i", i=4),
        )
        nc.scalar.activation(
            out=q_bf[:, 88:128, :].rearrange("p (c i) j -> p c j i", i=4),
            in_=q_raw[:, :, 88:128].rearrange("p j (c i) -> p c j i", i=4),
            func=ACT.Copy,
        )
        q_codes = sb.tile([P, Q], U32, name="q_codes", tag="codes_then_lam", align_bytes=64)
        q_scales = sb.tile([P, Q], U8, name="q_scales", tag="scales_then_averse", align_bytes=64)
        nc.vector.quantize_mx(
            out=q_codes[:].bitcast(FP8X4),
            scales=q_scales[:],
            in_=q_bf[:].rearrange("p q j -> p (q j)"),
        )

        old_t = sb.tile([P, T], F32, name="old_t", tag="raw_then_old")
        nc.sync.dma_start(out=old_t[:], in_=old)
        gain_t = sb.tile([P, I], F32, name="gain_t", tag="bf_then_gain", align_bytes=64)
        nc.sync.dma_start(out=gain_t[:], in_=gainm)

        a = sb.tile([P, T], F32, name="a", tag="a_then_gain")
        edges = (0, 512, 768, 896, 1024)
        for b in range(4):
            cols = slice(edges[b], edges[b + 1])
            bank = ps.tile([P, edges[b + 1] - edges[b]], F32, name="bank%d" % b)
            nc.tensor.matmul_mx(
                out=bank[:],
                lhsT=q_codes[:].bitcast(FP8X4),
                lhsT_scale=q_scales[:],
                rhs=k_words[edges[b] // 512][:, 2 * edges[b] % T : 2 * edges[b] % T + 2 * (edges[b + 1] - edges[b])].bitcast(FP4X4),
                rhs_scale=k_scales[:, cols],
                start=True,
                stop=True,
            )
            if b in (0, 3):
                nc.scalar.activation(out=a[:, cols], in_=bank[:], func=ACT.Copy)
            else:
                nc.vector.tensor_copy(out=a[:, cols], in_=bank[:])

        lam_t = sb.tile([P, 1], F32, name="lam_t", tag="codes_then_lam", align_bytes=64)
        nc.sync.dma_start(out=lam_t[:], in_=lam)
        averse_t = sb.tile([P, 1], F32, name="averse_t", tag="scales_then_averse", align_bytes=64)
        nc.sync.dma_start(out=averse_t[:], in_=averse)

        halves = [slice(0, HALF), slice(HALF, I)]
        list_halves = [slice(0, HALF // 16), slice(HALF // 16, I // 16)]

        x = sb.tile([P, I], F32, name="x")
        y = sb.tile([P, I], F32, name="y")
        z = sb.tile([P, I], F32, name="z")
        for h in range(2):
            nc.vector.tensor_copy(out=y[:, halves[h]], in_=a[:].indirect(lists[1][:, list_halves[h]]))
        for dst, lst in ((x, lists[0]), (z, lists[2])):
            for h in range(2):
                nc.scalar.activation(
                    out=dst[:, halves[h]], in_=a[:].indirect(lst[:, list_halves[h]]), func=ACT.Copy
                )

        gain256 = sb.tile([P, I], F32, name="gain256", tag="a_then_gain")
        nc.scalar.activation(out=gain256[:], in_=gain_t[:], func=ACT.Copy, scale=256.0)
        neg_lam = sb.tile([P, 1], F32, name="neg_lam")
        nc.scalar.activation(out=neg_lam[:], in_=lam_t[:], func=ACT.Copy, scale=-1.0)

        hi = sb.tile([P, I], F32, name="hi")
        lo = sb.tile([P, I], F32, name="lo")
        cap = sb.tile([P, I], F32, name="cap")
        mid = sb.tile([P, I], F32, name="mid")
        for h in halves:
            nc.vector.tensor_tensor(out=hi[:, h], in0=x[:, h], in1=y[:, h], op=ALU.max)
            nc.vector.tensor_tensor(out=lo[:, h], in0=x[:, h], in1=y[:, h], op=ALU.min)
        for h in halves:
            nc.vector.tensor_tensor(out=cap[:, h], in0=hi[:, h], in1=z[:, h], op=ALU.min)
        for h in halves:
            nc.vector.tensor_tensor(out=mid[:, h], in0=lo[:, h], in1=cap[:, h], op=ALU.max)

        s = sb.tile([P, I], F32, name="s")
        s_min = sb.tile([P, 1], F32, name="s_min")
        nc.vector.tensor_scalar(
            out=s[:], in0=mid[:], scalar1=lam_t[:], scalar2=None, op0=ALU.mult, op1=ALU.min, accum_out=s_min[:]
        )
        neg_max = sb.tile([P, 1], F32, name="neg_max")
        neg_s = sb.tile([P, I], F32, name="neg_s")
        nc.vector.tensor_scalar(
            out=neg_s[:], in0=mid[:], scalar1=neg_lam[:], scalar2=None, op0=ALU.mult, op1=ALU.min, accum_out=neg_max[:]
        )

        p2 = sb.tile([P, I], F32, name="p2")
        sum2 = sb.tile([P, 1], F32, name="sum2")
        nc.scalar.activation(out=p2[:], in_=s[:], func=ACT.Exp, bias=s_min[:], scale=-1.0, accum_out=sum2[:])
        p1 = sb.tile([P, I], F32, name="p1")
        sum1 = sb.tile([P, 1], F32, name="sum1")
        nc.scalar.activation(out=p1[:], in_=neg_s[:], func=ACT.Exp, bias=neg_max[:], scale=-1.0, accum_out=sum1[:])

        inv2 = sb.tile([P, 1], F32, name="inv2")
        nc.vector.reciprocal(out=inv2[:], in_=sum2[:])
        r2a = sb.tile([P, I], F32, name="r2a")
        nc.vector.tensor_scalar(
            out=r2a[:], in0=p2[:], scalar1=inv2[:], scalar2=averse_t[:], op0=ALU.mult, op1=ALU.mult
        )
        inv1 = sb.tile([P, 1], F32, name="inv1")
        nc.vector.reciprocal(out=inv1[:], in_=sum1[:])
        w = sb.tile([P, I], F32, name="w")
        nc.vector.scalar_tensor_tensor(
            out=w[:], in0=p1[:], scalar=inv1[:], in1=r2a[:], op0=ALU.mult, op1=ALU.subtract
        )
        nc.vector.tensor_tensor(out=wf[:].indirect(lists[3][:]), in0=w[:], in1=gain256[:], op=ALU.mult)

        out_edges = (0, 128, 384, 640, 896, 1024)
        for c in range(5):
            cols = slice(out_edges[c], out_edges[c + 1])
            res = sb.tile([P, out_edges[c + 1] - out_edges[c]], F32, name="res%d" % c)
            nc.vector.tensor_tensor(out=res[:], in0=old_t[:, cols], in1=wf[:, cols], op=ALU.add)
            queue = nc.sync if c % 2 == 0 else nc.scalar
            queue.dma_start(out=out[:, cols], in_=res[:])
